import numpy as np
import ml_dtypes


def mxq(x, axis, fmt="e4m3"):
    dtype, down = {"e4m3": (ml_dtypes.float8_e4m3fn, 7), "e5m2": (ml_dtypes.float8_e5m2, 14)}[fmt]
    v = np.moveaxis(np.asarray(x, np.float32).astype(ml_dtypes.bfloat16).astype(np.float64), axis, -1)
    blocks = v.reshape(v.shape[:-1] + (-1, 32))
    amax = np.abs(blocks).max(-1, keepdims=True)
    byte = np.maximum(np.where(amax > 0, np.frexp(amax)[1] - 1 + 127, 0) - down, 1)
    scale = np.exp2(byte - 127.0)
    codes = (blocks / scale).astype(np.float32).astype(dtype).astype(np.float64)
    return np.moveaxis((codes * scale).reshape(v.shape), -1, axis)


WIDE = False


def mx_kscale(k):
    if not WIDE:
        return np.ones(k)
    levels = np.array([10, -10, 5, -5, 0])
    if k % 512:
        return np.exp2(np.random.permutation(np.resize(levels, k // 32))).repeat(32)
    a = np.empty((k // 512, 16))
    for p in range(k // 512):
        a[p, :8] = np.random.permutation(np.resize(levels, 8))
        for g in range(8):
            far = levels[np.abs(levels - a[p, g]) >= 10]
            a[p, g + 8] = far[np.random.randint(len(far))]
    return np.exp2(a.ravel()).repeat(32)


def f64(x):
    return np.asarray(x).astype(np.float64)


def striped(idx):
    return np.tile(idx.reshape(-1, 16).T, (8, 1)).astype(np.uint16)


def unstriped(offs):
    return offs[:16].T.reshape(-1).astype(np.int64)


E2M1 = np.array([0.0, 0.5, 1.0, 1.5, 2.0, 3.0, 4.0, 6.0, -0.0, -0.5, -1.0, -1.5, -2.0, -3.0, -4.0, -6.0])


def pack_weight(w, fmt):
    k, n = w.shape
    w = f64(np.asarray(w, np.float32).astype(ml_dtypes.bfloat16)).reshape(k // 32, 32, n)
    amax = np.abs(w).max(1)
    if fmt == "e4m3":
        byte = np.frexp(amax)[1] - 1 + 127 - 7
    else:
        mant, ex = np.frexp(amax / 6.0)
        byte = np.where(mant > 0.5, ex, ex - 1) + 127
    byte = np.clip(np.where(amax > 0, byte, 1), 1, 254)
    scaled = (w * np.exp2(127.0 - byte)[:, None, :]).reshape(k, n).astype(np.float32)
    by_word = np.ascontiguousarray(scaled.reshape(k // 512, 128, 4, n).transpose(0, 1, 3, 2))
    if fmt == "e4m3":
        words = by_word.astype(ml_dtypes.float8_e4m3fn).view(np.uint8)
    else:
        c = by_word.astype(ml_dtypes.float4_e2m1fn).view(np.uint8) & 0xF
        words = (c[..., 0::2] | (c[..., 1::2] << 4)).reshape(k // 512, 128, 2 * n)
    return np.ascontiguousarray(words), np.ascontiguousarray(byte.astype(np.uint8).reshape(k // 512, 16, n))


def unpack_weight(words, scales, fmt):
    g, _, n = scales.shape
    words = np.ascontiguousarray(words).reshape(g, 128, n, -1)
    if fmt == "e4m3":
        vals = words.view(ml_dtypes.float8_e4m3fn).astype(np.float64)
    else:
        nib = np.empty((g, 128, n, 4), np.uint8)
        nib[..., 0::2] = words & 0xF
        nib[..., 1::2] = words >> 4
        vals = E2M1[nib]
    vals = vals * np.repeat(np.exp2(scales.astype(np.float64) - 127.0), 8, axis=1)[..., None]
    return vals.transpose(0, 1, 3, 2).reshape(g * 512, n)


def gelu(v):
    return 0.5 * v * (1.0 + np.tanh(np.sqrt(2.0 / np.pi) * (v + 0.044715 * v**3)))


K, H, N, M, T, S, T2, P = 1024, 512, 256, 256, 4096, 1024, 2048, 512


def setup_inputs():
    n = np.random.standard_normal
    s = mx_kscale(K)[:, None]
    u = mx_kscale(H)[:, None]
    tab_words, tab_scales = pack_weight(n((K, T)) * s, "e4m3")
    w2_words, w2_scales = pack_weight(0.55 * n((K, H)) / np.sqrt(K) / s * u.T, "e2m1")
    w4_words, w4_scales = pack_weight(0.45 * n((H, M)) / np.sqrt(H) / u, "e4m3")
    perm = np.random.permutation(T2)
    return {
        "tab_words": tab_words, "tab_scales": tab_scales,
        "offs": striped(np.random.permutation(T)[:S]),
        "offs2": striped(np.random.permutation(T2)[:S]),
        "offs3": striped(perm[:P]), "offs4": striped(perm[P:2 * P]),
        "w1": (1.6 * n((K, H)) / np.sqrt(K) / s).astype(np.float32),
        "gain": (0.9 * np.exp(0.3 * n(H)) * u[:, 0]).astype(np.float32),
        "w2_words": w2_words, "w2_scales": w2_scales,
        "page0": (n((H, T2)) * u).astype(np.float32),
        "wgs": np.exp(0.3 * n((128, S))).astype(np.float32),
        "cross": (0.6 * n((H, P))).astype(np.float32),
        "w3": (0.48 * n((H, N)) / np.sqrt(H) / u).astype(np.float32),
        "w4_words": w4_words, "w4_scales": w4_scales,
    }


def reference(tab_words, tab_scales, offs, offs2, offs3, offs4, w1, gain, w2_words, w2_scales,
              page0, wgs, cross, w3, w4_words, w4_scales):
    v = unpack_weight(tab_words, tab_scales, "e4m3")[:, unstriped(offs)]
    w2 = unpack_weight(w2_words, w2_scales, "e2m1")
    w4 = unpack_weight(w4_words, w4_scales, "e4m3")
    bent = np.tanh(mxq(f64(w1), 0, "e4m3").T @ v) * f64(gain)[:, None]
    h = bent + (w2.T @ v)
    page = f64(page0).copy()
    page[:, unstriped(offs2)] = np.tile(f64(wgs), (H // 128, 1)) * h
    a = page[:, unstriped(offs3)]
    b = page[:, unstriped(offs4)]
    page[:, unstriped(offs3)] = np.maximum(a, b)
    page[:, unstriped(offs4)] = a + f64(cross) * b
    pq = mxq(page, 0, "e4m3")
    out = np.zeros((N + M, T2))
    out[:N] = np.sin(mxq(f64(w3), 0, "e4m3").T @ pq)
    out[N:] = w4.T @ pq
    return out

@@ -1,0 +1,286 @@
+import math
+from contextlib import ExitStack
+
+import concourse.mybir as mybir
+
+K, H, N, M, T, S, T2, PAIRS = 1024, 512, 256, 256, 4096, 1024, 2048, 512
+FLOPS = 2 * (2 * K * H * S + H * (N + M) * T2)
+
+F32 = mybir.dt.float32
+BF16 = mybir.dt.bfloat16
+I32 = mybir.dt.int32
+U32 = mybir.dt.uint32
+U16 = mybir.dt.uint16
+U8 = mybir.dt.uint8
+FP8X4 = mybir.dt.float8_e4m3fn_x4
+FP4X4 = mybir.dt.float4_e2m1fn_x4
+ALU = mybir.AluOpType
+ACT = mybir.ActivationFunctionType
+
+P = 128
+PACK = 4
+PASSES = K // (P * PACK)
+BANK = 512
+QUADS = 4
+SLOT_ORDER = (2, 0, 1, 3)
+
+
+def tile_list_tram_junction_requests_kernel(
+    tc, tab_words, tab_scales, offs, offs2, offs3, offs4, w1, gain, w2_words, w2_scales,
+    page0, wgs, cross, w3, w4_words, w4_scales, out,
+):
+    nc = tc.nc
+    with ExitStack() as ctx:
+        lists = ctx.enter_context(tc.tile_pool(name="lists", bufs=1))
+        keep = ctx.enter_context(tc.tile_pool(name="keep", bufs=1))
+        work = ctx.enter_context(tc.tile_pool(name="work", bufs=2))
+        psum = ctx.enter_context(tc.psum_pool(name="psum", bufs=4))
+
+        idx = lists.tile([P, S // 16], U16, name="idx")
+        idx2 = lists.tile([P, S // 16], U16, name="idx2")
+        idx3 = lists.tile([P, PAIRS // 16], U16, name="idx3")
+        idx4 = lists.tile([P, PAIRS // 16], U16, name="idx4")
+
+        tab_sc = keep.tile([P, T // 4], I32, name="tab_sc", align_bytes=64)
+        w2_sc_raw = keep.tile([P, PASSES, H // 4], I32, name="w2_sc_raw", align_bytes=64)
+        v_sc = [keep.tile([P, S // 4], I32, name=f"v_sc{a}", align_bytes=64) for a in range(PASSES)]
+        w4_sc = keep.tile([P, M // 4], I32, name="w4_sc", align_bytes=64)
+        nc.vector.memset(tab_sc[:], 0)
+        nc.vector.memset(w2_sc_raw[:], 0)
+        for a in range(PASSES):
+            nc.vector.memset(v_sc[a][:], 0)
+        nc.vector.memset(w4_sc[:], 0)
+
+        tab = [keep.tile([P, T], I32, name=f"tab{a}", align_bytes=64) for a in range(PASSES)]
+        w1_raw = [keep.tile([P, PACK, H], F32, name=f"w1_raw{a}", tag="rows", bufs=3) for a in range(PASSES)]
+        w2_raw = keep.tile([P, PASSES, H // 2], I32, name="w2_raw", align_bytes=64)
+        gain_sb = keep.tile([P, PACK], F32, name="gain_sb")
+
+        def load_tab(a):
+            nc.sync.dma_start(out=tab[a][:], in_=tab_words[a].rearrange("p t i -> p (t i)").bitcast(I32))
+
+        nc.sync.dma_start(idx[:], offs)
+        load_tab(0)
+        nc.scalar.dma_start(out=tab_sc[0:P:4, :], in_=tab_scales.rearrange("a q t -> (a q) t").bitcast(I32))
+        nc.scalar.dma_start(out=w2_raw[:], in_=w2_words.rearrange("a p b -> p a b").bitcast(I32))
+        for q in range(QUADS):
+            nc.scalar.dma_start(
+                out=w2_sc_raw[32 * q : 32 * q + 4, :, :],
+                in_=w2_scales[:, 4 * q : 4 * q + 4, :].rearrange("a r c -> r a c").bitcast(I32),
+            )
+        for a in range(PASSES):
+            nc.sync.dma_start(
+                out=w1_raw[a][:], in_=w1[a * 512 : (a + 1) * 512, :].rearrange("(p j) c -> p j c", j=PACK)
+            )
+        load_tab(1)
+        nc.scalar.dma_start(out=gain_sb[:], in_=gain.rearrange("(p t) -> p t", t=PACK))
+
+        picked_sc = keep.tile([P, S // 4], I32, name="picked_sc", align_bytes=64)
+        nc.vector.tensor_copy(picked_sc[:].bitcast(U8), tab_sc[:].bitcast(U8).indirect(idx[:]))
+        for a in range(PASSES):
+            for r in range(4):
+                nc.scalar.dma_start(out=v_sc[a][r:P:32, :], in_=picked_sc[64 * a + 4 * r : 64 * a + 64 : 16, :])
+
+        pages = {}
+        page_rows = page0.rearrange("(p t) c -> t p c", t=PACK)
+        wgs_rows = wgs.rearrange("(m t) j -> m t j", t=PACK)
+
+        def load_page(t):
+            if t >= 2:
+                pages[t] = keep.tile([P, T2], F32, name=f"page{t}", tag="page_high", bufs=1)
+            else:
+                pages[t] = keep.tile([P, T2], F32, name=f"page{t}", tag="rows", bufs=3)
+            nc.sync.dma_start(out=pages[t][:], in_=page_rows[t])
+
+        weights = {}
+
+        def load_weight(t):
+            weights[t] = keep.tile([P, S], F32, name=f"weight{t}")
+            for q in range(QUADS):
+                nc.sync.dma_start(out=weights[t][32 * q : 32 * q + 32, :], in_=wgs_rows[:, t, :])
+
+        cross_sb = keep.tile([P, PACK, PAIRS], F32, name="cross_sb")
+        w3_raw = keep.tile([P, PACK, N], F32, name="w3_raw")
+        w4_codes = keep.tile([P, M], I32, name="w4_codes", align_bytes=64)
+
+        nc.sync.dma_start(idx2[:], offs2)
+        load_page(SLOT_ORDER[0])
+        load_weight(SLOT_ORDER[0])
+        nc.sync.dma_start(idx3[:], offs3)
+        nc.sync.dma_start(idx4[:], offs4)
+        nc.sync.dma_start(out=cross_sb[:], in_=cross.rearrange("(p t) j -> p t j", t=PACK))
+        load_page(SLOT_ORDER[1])
+        load_weight(SLOT_ORDER[1])
+
+        w2_codes = keep.tile([P, PASSES, 2 * H], U8, name="w2_codes", align_bytes=64)
+        w2_sc = keep.tile([P, PASSES, H], U8, name="w2_sc", align_bytes=64)
+        nc.vector.tensor_copy(
+            out=w2_codes[:].bitcast(U16).rearrange("p a (t m) -> p a t m", t=PACK),
+            in_=w2_raw[:].bitcast(U16).rearrange("p a (m t) -> p a t m", t=PACK),
+        )
+        nc.vector.tensor_copy(
+            out=w2_sc[:].rearrange("p a (t m) -> p a t m", t=PACK),
+            in_=w2_sc_raw[:].bitcast(U8).rearrange("p a (m t) -> p a t m", t=PACK),
+        )
+
+        halves = S // BANK
+        v_codes = {}
+
+        def gather_words(a, half):
+            v_codes[a, half] = keep.tile([P, BANK], U32, name=f"v_codes{a}{half}", align_bytes=64)
+            cols = slice(half * BANK // 16, (half + 1) * BANK // 16)
+            nc.vector.tensor_copy(v_codes[a, half][:], tab[a][:].bitcast(U32).indirect(idx[:, cols]))
+
+        for half in range(halves):
+            gather_words(0, half)
+
+        w1_codes = keep.tile([P, PASSES, H], U32, name="w1_codes", align_bytes=64)
+        w1_sc = keep.tile([P, PASSES, H], U8, name="w1_sc", align_bytes=64)
+        for a in range(PASSES):
+            w1_bf = keep.tile([P, PACK * H], BF16, name=f"w1_bf{a}", tag="grouped", bufs=4, align_bytes=64)
+            nc.scalar.copy(
+                out=w1_bf[:].rearrange("p (t m j) -> p m j t", t=PACK, j=PACK),
+                in_=w1_raw[a][:].rearrange("p j (m t) -> p m j t", t=PACK),
+            )
+            nc.vector.quantize_mx(out=w1_codes[:, a, :].bitcast(FP8X4), scales=w1_sc[:, a, :], in_=w1_bf[:])
+
+        for half in range(halves):
+            gather_words(1, half)
+
+        load_page(SLOT_ORDER[2])
+        load_weight(SLOT_ORDER[2])
+        load_weight(SLOT_ORDER[3])
+        nc.sync.dma_start(out=w3_raw[:], in_=w3.rearrange("(p j) n -> p j n", j=PACK))
+        nc.sync.dma_start(out=w4_codes[:], in_=w4_words[0].rearrange("p c i -> p (c i)").bitcast(I32))
+        for q in range(QUADS):
+            nc.sync.dma_start(out=w4_sc[32 * q : 32 * q + 4, :], in_=w4_scales[0, 4 * q : 4 * q + 4, :].bitcast(I32))
+
+
+        chunks = T2 // BANK
+        grouped = [
+            keep.tile([P, BANK, PACK], BF16, name=f"grouped{c}", tag="grouped", bufs=4, align_bytes=64)
+            for c in range(chunks)
+        ]
+
+        for step, t in enumerate(SLOT_ORDER):
+            page = pages[t]
+            weight = weights[t]
+            h = work.tile([P, S], F32, name="h", bufs=3)
+            for half in range(halves):
+                cols = slice(half * BANK, (half + 1) * BANK)
+                acc1 = psum.tile([P, BANK], F32, name="acc1", tag="left")
+                acc2 = psum.tile([P, BANK], F32, name="acc2", tag="right")
+                for a in range(PASSES):
+                    nc.tensor.matmul_mx(
+                        out=acc1[:],
+                        lhsT=w1_codes[:, a, t * P : (t + 1) * P].bitcast(FP8X4),
+                        lhsT_scale=w1_sc[:, a, t * P : (t + 1) * P],
+                        rhs=v_codes[a, half][:].bitcast(FP8X4),
+                        rhs_scale=v_sc[a][:].bitcast(U8)[:, cols],
+                        start=(a == 0),
+                        stop=(a == PASSES - 1),
+                    )
+                for a in range(PASSES):
+                    nc.tensor.matmul_mx(
+                        out=acc2[:],
+                        lhsT=w2_codes[:, a, 2 * t * P : 2 * (t + 1) * P].bitcast(FP4X4),
+                        lhsT_scale=w2_sc[:, a, t * P : (t + 1) * P],
+                        rhs=v_codes[a, half][:].bitcast(FP8X4),
+                        rhs_scale=v_sc[a][:].bitcast(U8)[:, cols],
+                        start=(a == 0),
+                        stop=(a == PASSES - 1),
+                    )
+                bent = work.tile([P, BANK], F32, name="bent", bufs=4)
+                nc.scalar.activation(out=bent[:], in_=acc1[:], func=ACT.Tanh)
+                nc.vector.scalar_tensor_tensor(
+                    out=h[:, cols], in0=bent[:], scalar=gain_sb[:, t : t + 1], in1=acc2[:], op0=ALU.mult, op1=ALU.add
+                )
+                if step == 0:
+                    part = slice(half * BANK // 16, (half + 1) * BANK // 16)
+                    nc.vector.tensor_tensor(page[:].indirect(idx2[:, part]), h[:, cols], weight[:, cols], ALU.mult)
+            if step > 0:
+                nc.vector.tensor_tensor(page[:].indirect(idx2[:]), h[:], weight[:], ALU.mult)
+
+            first = work.tile([P, PAIRS], F32, name="first")
+            second = work.tile([P, PAIRS], F32, name="second")
+            larger = work.tile([P, PAIRS], F32, name="larger")
+            crossed = work.tile([P, PAIRS], F32, name="crossed")
+            nc.vector.tensor_copy(second[:], page[:].indirect(idx4[:]))
+            nc.vector.tensor_copy(first[:], page[:].indirect(idx3[:]))
+            nc.vector.tensor_tensor(crossed[:], second[:], cross_sb[:, t, :], ALU.mult)
+            nc.vector.tensor_tensor(larger[:], first[:], second[:], ALU.max)
+            nc.vector.tensor_tensor(page[:].indirect(idx4[:]), first[:], crossed[:], ALU.add)
+            nc.vector.tensor_copy(page[:].indirect(idx3[:]), larger[:])
+            if step < PACK - 1:
+                for c in range(chunks):
+                    nc.scalar.copy(out=grouped[c][:, :, t], in_=page[:, c * BANK : (c + 1) * BANK])
+            if step == 0:
+                load_page(SLOT_ORDER[3])
+            if step == PACK - 2:
+                w3_bf = keep.tile([P, N, PACK], BF16, name="w3_bf", align_bytes=64)
+                w3_codes = keep.tile([P, N], U32, name="w3_codes", align_bytes=64)
+                w3_sc = keep.tile([P, N], U8, name="w3_sc", align_bytes=64)
+                nc.scalar.copy(
+                    out=w3_bf[:].rearrange("p (n i) j -> p n j i", i=4),
+                    in_=w3_raw[:].rearrange("p j (n i) -> p n j i", i=4),
+                )
+                nc.vector.quantize_mx(
+                    out=w3_codes[:].bitcast(FP8X4), scales=w3_sc[:], in_=w3_bf[:].rearrange("p n j -> p (n j)")
+                )
+
+        last = SLOT_ORDER[-1]
+        for c in range(chunks):
+            src = pages[last][:, c * BANK : (c + 1) * BANK]
+            if c % 2 == 0:
+                nc.vector.tensor_copy(out=grouped[c][:, :, last], in_=src)
+            else:
+                nc.scalar.copy(out=grouped[c][:, :, last], in_=src)
+        for c in range(chunks):
+            cols = slice(c * BANK, (c + 1) * BANK)
+            b_codes = work.tile([P, BANK], U32, name="b_codes", bufs=4, align_bytes=64)
+            b_sc = work.tile([P, BANK], U8, name="b_sc", bufs=4, align_bytes=64)
+            nc.vector.quantize_mx(
+                out=b_codes[:].bitcast(FP8X4), scales=b_sc[:], in_=grouped[c][:].rearrange("p c j -> p (c j)")
+            )
+            angles, plains = [], []
+            for nb in range(N // P):
+                angle = psum.tile([P, BANK], F32, name="angle", tag="left")
+                nc.tensor.matmul_mx(
+                    out=angle[:],
+                    lhsT=w3_codes[:, nb * P : (nb + 1) * P].bitcast(FP8X4),
+                    lhsT_scale=w3_sc[:, nb * P : (nb + 1) * P],
+                    rhs=b_codes[:].bitcast(FP8X4),
+                    rhs_scale=b_sc[:],
+                    start=True,
+                    stop=True,
+                )
+                angles.append(angle)
+            for mb in range(M // P):
+                plain = psum.tile([P, BANK], F32, name="plain", tag="right")
+                nc.tensor.matmul_mx(
+                    out=plain[:],
+                    lhsT=w4_codes[:, mb * P : (mb + 1) * P].bitcast(FP8X4),
+                    lhsT_scale=w4_sc[:].bitcast(U8)[:, mb * P : (mb + 1) * P],
+                    rhs=b_codes[:].bitcast(FP8X4),
+                    rhs_scale=b_sc[:],
+                    start=True,
+                    stop=True,
+                )
+                plains.append(plain)
+            turns = []
+            for angle in angles:
+                turn = work.tile([P, BANK], I32, name="turn", bufs=2)
+                nc.vector.tensor_scalar(turn[:], angle[:], 1.0 / (2.0 * math.pi), None, ALU.mult)
+                turns.append(turn)
+            for mb, plain in enumerate(plains):
+                staged = work.tile([P, BANK], F32, name="staged", bufs=6)
+                nc.scalar.copy(out=staged[:], in_=plain[:])
+                nc.sync.dma_start(out=out[N + mb * P : N + (mb + 1) * P, cols], in_=staged[:])
+            for nb, angle in enumerate(angles):
+                wrapped = work.tile([P, BANK], F32, name="wrapped", bufs=3)
+                nc.vector.scalar_tensor_tensor(
+                    out=wrapped[:], in0=turns[nb][:], scalar=-2.0 * math.pi, in1=angle[:], op0=ALU.mult, op1=ALU.add
+                )
+                staged = work.tile([P, BANK], F32, name="staged", bufs=6)
+                nc.scalar.activation(out=staged[:], in_=wrapped[:], func=ACT.Sin)
+                nc.sync.dma_start(out=out[nb * P : (nb + 1) * P, cols], in_=staged[:])

@@ -22,6 +22,8 @@ PACK = 4
 PASSES = K // (P * PACK)
 BANK = 512
 QUADS = 4
+SC_ROW = 32 - 4 * PASSES
+PLANE_ROWS = 100
 SLOT_ORDER = (2, 0, 1, 3)
 
 
@@ -36,35 +38,42 @@ def tile_list_tram_junction_requests_kernel(
         work = ctx.enter_context(tc.tile_pool(name="work", bufs=2))
         psum = ctx.enter_context(tc.psum_pool(name="psum", bufs=4))
 
+        def held(shape, dtype, name, tag=""):
+            return keep.tile(shape, dtype, name=name, tag=tag or name, align_bytes=64)
+
         idx = lists.tile([P, S // 16], U16, name="idx")
         idx2 = lists.tile([P, S // 16], U16, name="idx2")
         idx3 = lists.tile([P, PAIRS // 16], U16, name="idx3")
         idx4 = lists.tile([P, PAIRS // 16], U16, name="idx4")
 
-        tab_sc = keep.tile([P, T // 4], I32, name="tab_sc", align_bytes=64)
-        w2_sc_raw = keep.tile([P, PASSES, H // 4], I32, name="w2_sc_raw", align_bytes=64)
-        v_sc = [keep.tile([P, S // 4], I32, name=f"v_sc{a}", align_bytes=64) for a in range(PASSES)]
-        w4_sc = keep.tile([P, M // 4], I32, name="w4_sc", align_bytes=64)
-        nc.vector.memset(tab_sc[:], 0)
-        nc.vector.memset(w2_sc_raw[:], 0)
+        tab_sc = held([P, T // 4], I32, "tab_sc", "slot_a")
+        w2_sc_raw = held([P, PASSES, H // 4], I32, "w2_sc_raw")
+        v_sc = [held([P, S // 4], I32, f"v_sc{a}") for a in range(PASSES)]
+        w4_sc = held([P, M // 4], I32, "w4_sc")
+        for q in range(QUADS):
+            nc.vector.memset(tab_sc[32 * q : 32 * q + SC_ROW, :], 0)
+        nc.gpsimd.memset(w2_sc_raw[:], 0)
         for a in range(PASSES):
-            nc.vector.memset(v_sc[a][:], 0)
-        nc.vector.memset(w4_sc[:], 0)
+            nc.gpsimd.memset(v_sc[a][:], 0)
+        nc.gpsimd.memset(w4_sc[:], 0)
 
-        tab = [keep.tile([P, T], I32, name=f"tab{a}", align_bytes=64) for a in range(PASSES)]
-        w1_raw = [keep.tile([P, PACK, H], F32, name=f"w1_raw{a}", tag="rows", bufs=3) for a in range(PASSES)]
-        w2_raw = keep.tile([P, PASSES, H // 2], I32, name="w2_raw", align_bytes=64)
-        gain_sb = keep.tile([P, PACK], F32, name="gain_sb")
+        tab = {}
+        w1_raw = [held([P, PACK, H], F32, "w1_raw0", "slot_b"), held([P, PACK, H], F32, "w1_raw1", "slot_c")]
+        w2_raw = held([P, PASSES, H // 2], I32, "w2_raw")
+        gain_sb = held([P, PACK], F32, "gain_sb")
 
-        def load_tab(a):
+        def load_tab(a, slot):
+            tab[a] = held([P, T], I32, f"tab{a}", slot)
             nc.sync.dma_start(out=tab[a][:], in_=tab_words[a].rearrange("p t i -> p (t i)").bitcast(I32))
 
         nc.sync.dma_start(idx[:], offs)
-        load_tab(0)
-        nc.scalar.dma_start(out=tab_sc[0:P:4, :], in_=tab_scales.rearrange("a q t -> (a q) t").bitcast(I32))
-        nc.scalar.dma_start(out=w2_raw[:], in_=w2_words.rearrange("a p b -> p a b").bitcast(I32))
         for q in range(QUADS):
-            nc.scalar.dma_start(
+            nc.sync.dma_start(
+                out=tab_sc[32 * q + SC_ROW : 32 * q + 32, :], in_=tab_scales[:, 4 * q : 4 * q + 4, :].bitcast(I32)
+            )
+        load_tab(0, "slot_d")
+        for q in range(QUADS):
+            nc.gpsimd.dma_start(
                 out=w2_sc_raw[32 * q : 32 * q + 4, :, :],
                 in_=w2_scales[:, 4 * q : 4 * q + 4, :].rearrange("a r c -> r a c").bitcast(I32),
             )
@@ -72,48 +81,56 @@ def tile_list_tram_junction_requests_kernel(
             nc.sync.dma_start(
                 out=w1_raw[a][:], in_=w1[a * 512 : (a + 1) * 512, :].rearrange("(p j) c -> p j c", j=PACK)
             )
-        load_tab(1)
-        nc.scalar.dma_start(out=gain_sb[:], in_=gain.rearrange("(p t) -> p t", t=PACK))
+        nc.sync.dma_start(out=w2_raw[:], in_=w2_words.rearrange("a p b -> p a b").bitcast(I32))
+        nc.gpsimd.dma_start(out=gain_sb[:], in_=gain.rearrange("(p t) -> p t", t=PACK))
+        for q in range(QUADS):
+            nc.gpsimd.dma_start(out=w4_sc[32 * q : 32 * q + 4, :], in_=w4_scales[0, 4 * q : 4 * q + 4, :].bitcast(I32))
 
-        picked_sc = keep.tile([P, S // 4], I32, name="picked_sc", align_bytes=64)
-        nc.vector.tensor_copy(picked_sc[:].bitcast(U8), tab_sc[:].bitcast(U8).indirect(idx[:]))
-        for a in range(PASSES):
-            for r in range(4):
-                nc.scalar.dma_start(out=v_sc[a][r:P:32, :], in_=picked_sc[64 * a + 4 * r : 64 * a + 64 : 16, :])
-
-        pages = {}
+        pages, weights = {}, {}
         page_rows = page0.rearrange("(p t) c -> t p c", t=PACK)
         wgs_rows = wgs.rearrange("(m t) j -> m t j", t=PACK)
 
-        def load_page(t):
-            if t >= 2:
-                pages[t] = keep.tile([P, T2], F32, name=f"page{t}", tag="page_high", bufs=1)
-            else:
-                pages[t] = keep.tile([P, T2], F32, name=f"page{t}", tag="rows", bufs=3)
+        def load_page(t, slot):
+            pages[t] = held([P, T2], F32, f"page{t}", slot)
             nc.sync.dma_start(out=pages[t][:], in_=page_rows[t])
 
-        weights = {}
-
-        def load_weight(t):
-            weights[t] = keep.tile([P, S], F32, name=f"weight{t}")
+        def load_weight(t, slot):
+            weights[t] = held([P, S], F32, f"weight{t}", slot)
             for q in range(QUADS):
                 nc.sync.dma_start(out=weights[t][32 * q : 32 * q + 32, :], in_=wgs_rows[:, t, :])
 
-        cross_sb = keep.tile([P, PACK, PAIRS], F32, name="cross_sb")
-        w3_raw = keep.tile([P, PACK, N], F32, name="w3_raw")
-        w4_codes = keep.tile([P, M], I32, name="w4_codes", align_bytes=64)
+        halves = S // BANK
+        v_codes = {}
 
+        def gather_words(a, half):
+            v_codes[a, half] = held([P, BANK], U32, f"v_codes{a}{half}")
+            cols = slice(half * BANK // 16, (half + 1) * BANK // 16)
+            nc.vector.tensor_copy(v_codes[a, half][:], tab[a][:].bitcast(U32).indirect(idx[:, cols]))
+
+        picked_sc = held([P, S // 4], I32, "picked_sc", "slot_e")
+        nc.vector.tensor_copy(picked_sc[:].bitcast(U8), tab_sc[:].bitcast(U8).indirect(idx[:]))
+        for a in range(PASSES):
+            row = SC_ROW + 4 * a
+            nc.sync.dma_start(out=v_sc[a][0:PLANE_ROWS, :], in_=picked_sc[row : row + PLANE_ROWS, :])
+        load_tab(1, "slot_a")
         nc.sync.dma_start(idx2[:], offs2)
-        load_page(SLOT_ORDER[0])
-        load_weight(SLOT_ORDER[0])
-        nc.sync.dma_start(idx3[:], offs3)
-        nc.sync.dma_start(idx4[:], offs4)
-        nc.sync.dma_start(out=cross_sb[:], in_=cross.rearrange("(p t) j -> p t j", t=PACK))
-        load_page(SLOT_ORDER[1])
-        load_weight(SLOT_ORDER[1])
 
-        w2_codes = keep.tile([P, PASSES, 2 * H], U8, name="w2_codes", align_bytes=64)
-        w2_sc = keep.tile([P, PASSES, H], U8, name="w2_sc", align_bytes=64)
+        for half in range(halves):
+            gather_words(0, half)
+        load_page(SLOT_ORDER[0], "slot_d")
+
+        w1_codes = held([P, PASSES, H], U32, "w1_codes")
+        w1_sc = held([P, PASSES, H], U8, "w1_sc")
+        for a in range(PASSES):
+            w1_bf = held([P, PACK * H], BF16, f"w1_bf{a}", ("slot_f", "slot_g")[a])
+            nc.scalar.copy(
+                out=w1_bf[:].rearrange("p (t m j) -> p m j t", t=PACK, j=PACK),
+                in_=w1_raw[a][:].rearrange("p j (m t) -> p m j t", t=PACK),
+            )
+            nc.vector.quantize_mx(out=w1_codes[:, a, :].bitcast(FP8X4), scales=w1_sc[:, a, :], in_=w1_bf[:])
+
+        w2_codes = held([P, PASSES, 2 * H], U8, "w2_codes")
+        w2_sc = held([P, PASSES, H], U8, "w2_sc", "slot_e")
         nc.vector.tensor_copy(
             out=w2_codes[:].bitcast(U16).rearrange("p a (t m) -> p a t m", t=PACK),
             in_=w2_raw[:].bitcast(U16).rearrange("p a (m t) -> p a t m", t=PACK),
@@ -123,44 +140,21 @@ def tile_list_tram_junction_requests_kernel(
             in_=w2_sc_raw[:].bitcast(U8).rearrange("p a (m t) -> p a t m", t=PACK),
         )
 
-        halves = S // BANK
-        v_codes = {}
-
-        def gather_words(a, half):
-            v_codes[a, half] = keep.tile([P, BANK], U32, name=f"v_codes{a}{half}", align_bytes=64)
-            cols = slice(half * BANK // 16, (half + 1) * BANK // 16)
-            nc.vector.tensor_copy(v_codes[a, half][:], tab[a][:].bitcast(U32).indirect(idx[:, cols]))
-
-        for half in range(halves):
-            gather_words(0, half)
-
-        w1_codes = keep.tile([P, PASSES, H], U32, name="w1_codes", align_bytes=64)
-        w1_sc = keep.tile([P, PASSES, H], U8, name="w1_sc", align_bytes=64)
-        for a in range(PASSES):
-            w1_bf = keep.tile([P, PACK * H], BF16, name=f"w1_bf{a}", tag="grouped", bufs=4, align_bytes=64)
-            nc.scalar.copy(
-                out=w1_bf[:].rearrange("p (t m j) -> p m j t", t=PACK, j=PACK),
-                in_=w1_raw[a][:].rearrange("p j (m t) -> p m j t", t=PACK),
-            )
-            nc.vector.quantize_mx(out=w1_codes[:, a, :].bitcast(FP8X4), scales=w1_sc[:, a, :], in_=w1_bf[:])
-
         for half in range(halves):
             gather_words(1, half)
 
-        load_page(SLOT_ORDER[2])
-        load_weight(SLOT_ORDER[2])
-        load_weight(SLOT_ORDER[3])
+        load_weight(SLOT_ORDER[0], "slot_b")
+        nc.sync.dma_start(idx4[:], offs4)
+        nc.sync.dma_start(idx3[:], offs3)
+        w3_raw = held([P, PACK, N], F32, "w3_raw", "slot_f")
         nc.sync.dma_start(out=w3_raw[:], in_=w3.rearrange("(p j) n -> p j n", j=PACK))
-        nc.sync.dma_start(out=w4_codes[:], in_=w4_words[0].rearrange("p c i -> p (c i)").bitcast(I32))
-        for q in range(QUADS):
-            nc.sync.dma_start(out=w4_sc[32 * q : 32 * q + 4, :], in_=w4_scales[0, 4 * q : 4 * q + 4, :].bitcast(I32))
-
+        cross_sb = held([P, PACK, PAIRS], F32, "cross_sb", "slot_c")
+        nc.sync.dma_start(out=cross_sb[:], in_=cross.rearrange("(p t) j -> p t j", t=PACK))
+        load_weight(SLOT_ORDER[1], "slot_g")
+        load_page(SLOT_ORDER[1], "slot_a")
 
         chunks = T2 // BANK
-        grouped = [
-            keep.tile([P, BANK, PACK], BF16, name=f"grouped{c}", tag="grouped", bufs=4, align_bytes=64)
-            for c in range(chunks)
-        ]
+        grouped = [held([P, BANK, PACK], BF16, f"grouped{c}") for c in range(chunks)]
 
         for step, t in enumerate(SLOT_ORDER):
             page = pages[t]
@@ -190,7 +184,7 @@ def tile_list_tram_junction_requests_kernel(
                         start=(a == 0),
                         stop=(a == PASSES - 1),
                     )
-                bent = work.tile([P, BANK], F32, name="bent", bufs=4)
+                bent = work.tile([P, BANK], F32, name="bent", bufs=8)
                 nc.scalar.activation(out=bent[:], in_=acc1[:], func=ACT.Tanh)
                 nc.vector.scalar_tensor_tensor(
                     out=h[:, cols], in0=bent[:], scalar=gain_sb[:, t : t + 1], in1=acc2[:], op0=ALU.mult, op1=ALU.add
@@ -200,6 +194,24 @@ def tile_list_tram_junction_requests_kernel(
                     nc.vector.tensor_tensor(page[:].indirect(idx2[:, part]), h[:, cols], weight[:, cols], ALU.mult)
             if step > 0:
                 nc.vector.tensor_tensor(page[:].indirect(idx2[:]), h[:], weight[:], ALU.mult)
+            if step == 0:
+                w3_bf = held([P, N, PACK], BF16, "w3_bf")
+                w3_codes = held([P, N], U32, "w3_codes")
+                w3_sc = held([P, N], U8, "w3_sc")
+                nc.scalar.copy(
+                    out=w3_bf[:].rearrange("p (n i) j -> p n j i", i=4),
+                    in_=w3_raw[:].rearrange("p j (n i) -> p n j i", i=4),
+                )
+                nc.vector.quantize_mx(
+                    out=w3_codes[:].bitcast(FP8X4), scales=w3_sc[:], in_=w3_bf[:].rearrange("p n j -> p (n j)")
+                )
+                load_page(SLOT_ORDER[2], "slot_f")
+                load_weight(SLOT_ORDER[2], "slot_b")
+            if step == 1:
+                load_weight(SLOT_ORDER[3], "slot_g")
+            if step == 2:
+                w4_codes = held([P, M], I32, "w4_codes", "slot_b")
+                nc.sync.dma_start(out=w4_codes[:], in_=w4_words[0].rearrange("p c i -> p (c i)").bitcast(I32))
 
             first = work.tile([P, PAIRS], F32, name="first")
             second = work.tile([P, PAIRS], F32, name="second")
@@ -215,18 +227,7 @@ def tile_list_tram_junction_requests_kernel(
                 for c in range(chunks):
                     nc.scalar.copy(out=grouped[c][:, :, t], in_=page[:, c * BANK : (c + 1) * BANK])
             if step == 0:
-                load_page(SLOT_ORDER[3])
-            if step == PACK - 2:
-                w3_bf = keep.tile([P, N, PACK], BF16, name="w3_bf", align_bytes=64)
-                w3_codes = keep.tile([P, N], U32, name="w3_codes", align_bytes=64)
-                w3_sc = keep.tile([P, N], U8, name="w3_sc", align_bytes=64)
-                nc.scalar.copy(
-                    out=w3_bf[:].rearrange("p (n i) j -> p n j i", i=4),
-                    in_=w3_raw[:].rearrange("p j (n i) -> p n j i", i=4),
-                )
-                nc.vector.quantize_mx(
-                    out=w3_codes[:].bitcast(FP8X4), scales=w3_sc[:], in_=w3_bf[:].rearrange("p n j -> p (n j)")
-                )
+                load_page(SLOT_ORDER[3], "slot_d")
 
         last = SLOT_ORDER[-1]
         for c in range(chunks):

@@ -2,6 +2,7 @@ import math
 from contextlib import ExitStack
 
 import concourse.mybir as mybir
+from concourse.masks import make_identity
 
 K, H, N, M, T, S, T2, PAIRS = 1024, 512, 256, 256, 4096, 1024, 2048, 512
 FLOPS = 2 * (2 * K * H * S + H * (N + M) * T2)
@@ -86,6 +87,11 @@ def tile_list_tram_junction_requests_kernel(
         for q in range(QUADS):
             nc.gpsimd.dma_start(out=w4_sc[32 * q : 32 * q + 4, :], in_=w4_scales[0, 4 * q : 4 * q + 4, :].bitcast(I32))
 
+        identity = held([P, P], F32, "identity")
+        make_identity(nc, identity[:])
+        planes = held([P, PACK, T2], BF16, "planes")
+        nc.gpsimd.memset(planes[:, SLOT_ORDER[-1], :], 0.0)
+
         pages, weights = {}, {}
         page_rows = page0.rearrange("(p t) c -> t p c", t=PACK)
         wgs_rows = wgs.rearrange("(m t) j -> m t j", t=PACK)
@@ -96,7 +102,7 @@ def tile_list_tram_junction_requests_kernel(
 
         def load_weight(t, slot):
             weights[t] = held([P, S], F32, f"weight{t}", slot)
-            for q in range(QUADS):
+            for q in (0, 2, 1, 3):
                 nc.sync.dma_start(out=weights[t][32 * q : 32 * q + 32, :], in_=wgs_rows[:, t, :])
 
         halves = S // BANK
@@ -124,8 +130,8 @@ def tile_list_tram_junction_requests_kernel(
         for a in range(PASSES):
             w1_bf = held([P, PACK * H], BF16, f"w1_bf{a}", ("slot_f", "slot_g")[a])
             nc.scalar.copy(
-                out=w1_bf[:].rearrange("p (t m j) -> p m j t", t=PACK, j=PACK),
-                in_=w1_raw[a][:].rearrange("p j (m t) -> p m j t", t=PACK),
+                out=w1_bf[:].rearrange("p (t m j) -> p m t j", t=PACK, j=PACK),
+                in_=w1_raw[a][:].rearrange("p j (m t) -> p m t j", t=PACK),
             )
             nc.vector.quantize_mx(out=w1_codes[:, a, :].bitcast(FP8X4), scales=w1_sc[:, a, :], in_=w1_bf[:])
 
@@ -156,44 +162,76 @@ def tile_list_tram_junction_requests_kernel(
         chunks = T2 // BANK
         grouped = [held([P, BANK, PACK], BF16, f"grouped{c}") for c in range(chunks)]
 
+        def products(t, half):
+            cols = slice(half * BANK, (half + 1) * BANK)
+            acc1 = psum.tile([P, BANK], F32, name="acc1", tag="left")
+            acc2 = psum.tile([P, BANK], F32, name="acc2", tag="right")
+            for a in range(PASSES):
+                nc.tensor.matmul_mx(
+                    out=acc1[:],
+                    lhsT=w1_codes[:, a, t * P : (t + 1) * P].bitcast(FP8X4),
+                    lhsT_scale=w1_sc[:, a, t * P : (t + 1) * P],
+                    rhs=v_codes[a, half][:].bitcast(FP8X4),
+                    rhs_scale=v_sc[a][:].bitcast(U8)[:, cols],
+                    start=(a == 0),
+                    stop=(a == PASSES - 1),
+                )
+            for a in range(PASSES):
+                nc.tensor.matmul_mx(
+                    out=acc2[:],
+                    lhsT=w2_codes[:, a, 2 * t * P : 2 * (t + 1) * P].bitcast(FP4X4),
+                    lhsT_scale=w2_sc[:, a, t * P : (t + 1) * P],
+                    rhs=v_codes[a, half][:].bitcast(FP8X4),
+                    rhs_scale=v_sc[a][:].bitcast(U8)[:, cols],
+                    start=(a == 0),
+                    stop=(a == PASSES - 1),
+                )
+            bent = work.tile([P, BANK], F32, name="bent", bufs=3)
+            nc.scalar.activation(out=bent[:], in_=acc1[:], func=ACT.Tanh)
+            return bent, acc2
+
+        def sum_on_tensor(t, bent, acc2, target):
+            gained = work.tile([P, BANK], F32, name="gained")
+            linear = work.tile([P, BANK], F32, name="linear")
+            turned = work.tile([P, BANK], F32, name="turned")
+            nc.scalar.activation(out=gained[:], in_=bent[:], func=ACT.Copy, scale=gain_sb[:, t : t + 1])
+            nc.scalar.copy(out=linear[:], in_=acc2[:])
+            summed = psum.tile([P, BANK], F32, name="summed", tag="left")
+            for blk in range(BANK // P):
+                cols = slice(blk * P, (blk + 1) * P)
+                for term, opens in ((gained, True), (linear, False)):
+                    nc.tensor.matmul(
+                        summed[:, cols], term[:, cols], identity[:], start=opens, stop=not opens, is_transpose=True
+                    )
+            nc.scalar.copy(out=turned[:], in_=summed[:])
+            back = psum.tile([P, BANK], F32, name="back", tag="right")
+            for blk in range(BANK // P):
+                cols = slice(blk * P, (blk + 1) * P)
+                nc.tensor.transpose(back[:, cols], turned[:, cols], identity[:])
+            nc.scalar.copy(out=target, in_=back[:])
+
+        requests = {t: held([P, S], F32, f"request{t}") for t in SLOT_ORDER}
+        t = SLOT_ORDER[0]
+        for half in range(halves):
+            cols = slice(half * BANK, (half + 1) * BANK)
+            part = slice(half * BANK // 16, (half + 1) * BANK // 16)
+            bent, acc2 = products(t, half)
+            nc.vector.scalar_tensor_tensor(
+                out=requests[t][:, cols], in0=bent[:], scalar=gain_sb[:, t : t + 1], in1=acc2[:],
+                op0=ALU.mult, op1=ALU.add,
+            )
+            nc.vector.tensor_tensor(
+                pages[t][:].indirect(idx2[:, part]), requests[t][:, cols], weights[t][:, cols], ALU.mult
+            )
+        for t in SLOT_ORDER[1:]:
+            for half in range(halves):
+                bent, acc2 = products(t, half)
+                sum_on_tensor(t, bent, acc2, requests[t][:, half * BANK : (half + 1) * BANK])
+
         for step, t in enumerate(SLOT_ORDER):
             page = pages[t]
-            weight = weights[t]
-            h = work.tile([P, S], F32, name="h", bufs=3)
-            for half in range(halves):
-                cols = slice(half * BANK, (half + 1) * BANK)
-                acc1 = psum.tile([P, BANK], F32, name="acc1", tag="left")
-                acc2 = psum.tile([P, BANK], F32, name="acc2", tag="right")
-                for a in range(PASSES):
-                    nc.tensor.matmul_mx(
-                        out=acc1[:],
-                        lhsT=w1_codes[:, a, t * P : (t + 1) * P].bitcast(FP8X4),
-                        lhsT_scale=w1_sc[:, a, t * P : (t + 1) * P],
-                        rhs=v_codes[a, half][:].bitcast(FP8X4),
-                        rhs_scale=v_sc[a][:].bitcast(U8)[:, cols],
-                        start=(a == 0),
-                        stop=(a == PASSES - 1),
-                    )
-                for a in range(PASSES):
-                    nc.tensor.matmul_mx(
-                        out=acc2[:],
-                        lhsT=w2_codes[:, a, 2 * t * P : 2 * (t + 1) * P].bitcast(FP4X4),
-                        lhsT_scale=w2_sc[:, a, t * P : (t + 1) * P],
-                        rhs=v_codes[a, half][:].bitcast(FP8X4),
-                        rhs_scale=v_sc[a][:].bitcast(U8)[:, cols],
-                        start=(a == 0),
-                        stop=(a == PASSES - 1),
-                    )
-                bent = work.tile([P, BANK], F32, name="bent", bufs=8)
-                nc.scalar.activation(out=bent[:], in_=acc1[:], func=ACT.Tanh)
-                nc.vector.scalar_tensor_tensor(
-                    out=h[:, cols], in0=bent[:], scalar=gain_sb[:, t : t + 1], in1=acc2[:], op0=ALU.mult, op1=ALU.add
-                )
-                if step == 0:
-                    part = slice(half * BANK // 16, (half + 1) * BANK // 16)
-                    nc.vector.tensor_tensor(page[:].indirect(idx2[:, part]), h[:, cols], weight[:, cols], ALU.mult)
             if step > 0:
-                nc.vector.tensor_tensor(page[:].indirect(idx2[:]), h[:], weight[:], ALU.mult)
+                nc.vector.tensor_tensor(page[:].indirect(idx2[:]), requests[t][:], weights[t][:], ALU.mult)
             if step == 0:
                 w3_bf = held([P, N, PACK], BF16, "w3_bf")
                 w3_codes = held([P, N], U32, "w3_codes")
@@ -224,8 +262,13 @@ def tile_list_tram_junction_requests_kernel(
             nc.vector.tensor_tensor(page[:].indirect(idx4[:]), first[:], crossed[:], ALU.add)
             nc.vector.tensor_copy(page[:].indirect(idx3[:]), larger[:])
             if step < PACK - 1:
+                nc.scalar.copy(out=planes[:, t, :], in_=page[:])
+            if step == PACK - 2:
                 for c in range(chunks):
-                    nc.scalar.copy(out=grouped[c][:, :, t], in_=page[:, c * BANK : (c + 1) * BANK])
+                    nc.scalar.copy(
+                        out=grouped[c][:].rearrange("p (c i) t -> p c t i", i=4),
+                        in_=planes[:, :, c * BANK : (c + 1) * BANK].rearrange("p t (c i) -> p c t i", i=4),
+                    )
             if step == 0:
                 load_page(SLOT_ORDER[3], "slot_d")
 

@@ -89,8 +89,6 @@ def tile_list_tram_junction_requests_kernel(
 
         identity = held([P, P], F32, "identity")
         make_identity(nc, identity[:])
-        planes = held([P, PACK, T2], BF16, "planes")
-        nc.gpsimd.memset(planes[:, SLOT_ORDER[-1], :], 0.0)
 
         pages, weights = {}, {}
         page_rows = page0.rearrange("(p t) c -> t p c", t=PACK)
@@ -104,6 +102,13 @@ def tile_list_tram_junction_requests_kernel(
             weights[t] = held([P, S], F32, f"weight{t}", slot)
             for q in (0, 2, 1, 3):
                 nc.sync.dma_start(out=weights[t][32 * q : 32 * q + 32, :], in_=wgs_rows[:, t, :])
+
+        crosses = {}
+        cross_rows = cross.rearrange("(p t) j -> t p j", t=PACK)
+
+        def load_cross(t):
+            crosses[t] = held([P, PAIRS], F32, f"cross{t}")
+            nc.sync.dma_start(out=crosses[t][:], in_=cross_rows[t])
 
         halves = S // BANK
         v_codes = {}
@@ -154,10 +159,9 @@ def tile_list_tram_junction_requests_kernel(
         nc.sync.dma_start(idx3[:], offs3)
         w3_raw = held([P, PACK, N], F32, "w3_raw", "slot_f")
         nc.sync.dma_start(out=w3_raw[:], in_=w3.rearrange("(p j) n -> p j n", j=PACK))
-        cross_sb = held([P, PACK, PAIRS], F32, "cross_sb", "slot_c")
-        nc.sync.dma_start(out=cross_sb[:], in_=cross.rearrange("(p t) j -> p t j", t=PACK))
         load_weight(SLOT_ORDER[1], "slot_g")
         load_page(SLOT_ORDER[1], "slot_a")
+        load_cross(SLOT_ORDER[0])
 
         chunks = T2 // BANK
         grouped = [held([P, BANK, PACK], BF16, f"grouped{c}") for c in range(chunks)]
@@ -245,8 +249,12 @@ def tile_list_tram_junction_requests_kernel(
                 )
                 load_page(SLOT_ORDER[2], "slot_f")
                 load_weight(SLOT_ORDER[2], "slot_b")
+                load_cross(SLOT_ORDER[1])
             if step == 1:
                 load_weight(SLOT_ORDER[3], "slot_g")
+                load_page(SLOT_ORDER[3], "slot_d")
+                load_cross(SLOT_ORDER[2])
+                load_cross(SLOT_ORDER[3])
             if step == 2:
                 w4_codes = held([P, M], I32, "w4_codes", "slot_b")
                 nc.sync.dma_start(out=w4_codes[:], in_=w4_words[0].rearrange("p c i -> p (c i)").bitcast(I32))
@@ -257,20 +265,13 @@ def tile_list_tram_junction_requests_kernel(
             crossed = work.tile([P, PAIRS], F32, name="crossed")
             nc.vector.tensor_copy(second[:], page[:].indirect(idx4[:]))
             nc.vector.tensor_copy(first[:], page[:].indirect(idx3[:]))
-            nc.vector.tensor_tensor(crossed[:], second[:], cross_sb[:, t, :], ALU.mult)
+            nc.vector.tensor_tensor(crossed[:], second[:], crosses[t][:], ALU.mult)
             nc.vector.tensor_tensor(larger[:], first[:], second[:], ALU.max)
             nc.vector.tensor_tensor(page[:].indirect(idx4[:]), first[:], crossed[:], ALU.add)
             nc.vector.tensor_copy(page[:].indirect(idx3[:]), larger[:])
             if step < PACK - 1:
-                nc.scalar.copy(out=planes[:, t, :], in_=page[:])
-            if step == PACK - 2:
                 for c in range(chunks):
-                    nc.scalar.copy(
-                        out=grouped[c][:].rearrange("p (c i) t -> p c t i", i=4),
-                        in_=planes[:, :, c * BANK : (c + 1) * BANK].rearrange("p t (c i) -> p c t i", i=4),
-                    )
-            if step == 0:
-                load_page(SLOT_ORDER[3], "slot_d")
+                    nc.scalar.copy(out=grouped[c][:, :, t], in_=page[:, c * BANK : (c + 1) * BANK])
 
         last = SLOT_ORDER[-1]
         for c in range(chunks):

@@ -20,12 +20,19 @@ ACT = mybir.ActivationFunctionType
 
 P = 128
 PACK = 4
-PASSES = K // (P * PACK)
+K_PASS = P * PACK
+PASSES = K // K_PASS
 BANK = 512
 QUADS = 4
-SC_ROW = 32 - 4 * PASSES
-PLANE_ROWS = 100
+QUAD = P // QUADS
+LIVE = 4
+PER_COLUMN = 16
+HALVES = S // BANK
+CHUNKS = T2 // BANK
+SCALE_ROW0 = P - PASSES * QUADS * LIVE
+EARLY_MOVES = 6
 SLOT_ORDER = (2, 0, 1, 3)
+QUAD_ORDER = (0, 2, 1, 3)
 
 
 def tile_list_tram_junction_requests_kernel(
@@ -39,101 +46,101 @@ def tile_list_tram_junction_requests_kernel(
         work = ctx.enter_context(tc.tile_pool(name="work", bufs=2))
         psum = ctx.enter_context(tc.psum_pool(name="psum", bufs=4))
 
-        def held(shape, dtype, name, tag=""):
-            return keep.tile(shape, dtype, name=name, tag=tag or name, align_bytes=64)
+        def held(shape, dtype, name, buffer=""):
+            return keep.tile(shape, dtype, name=name, tag=buffer or name, align_bytes=64)
 
-        idx = lists.tile([P, S // 16], U16, name="idx")
-        idx2 = lists.tile([P, S // 16], U16, name="idx2")
-        idx3 = lists.tile([P, PAIRS // 16], U16, name="idx3")
-        idx4 = lists.tile([P, PAIRS // 16], U16, name="idx4")
+        def entries(half):
+            return slice(half * BANK // PER_COLUMN, (half + 1) * BANK // PER_COLUMN)
 
-        tab_sc = held([P, T // 4], I32, "tab_sc", "slot_a")
+        idx = lists.tile([P, S // PER_COLUMN], U16, name="idx")
+        idx2 = lists.tile([P, S // PER_COLUMN], U16, name="idx2")
+        idx3 = lists.tile([P, PAIRS // PER_COLUMN], U16, name="idx3")
+        idx4 = lists.tile([P, PAIRS // PER_COLUMN], U16, name="idx4")
+
+        tab_sc = held([P, T // 4], I32, "tab_sc", "buffer_e")
         w2_sc_raw = held([P, PASSES, H // 4], I32, "w2_sc_raw")
         v_sc = [held([P, S // 4], I32, f"v_sc{a}") for a in range(PASSES)]
         w4_sc = held([P, M // 4], I32, "w4_sc")
-        for q in range(QUADS):
-            nc.vector.memset(tab_sc[32 * q : 32 * q + SC_ROW, :], 0)
+        nc.vector.memset(tab_sc[0:SCALE_ROW0, :], 0)
         nc.gpsimd.memset(w2_sc_raw[:], 0)
         for a in range(PASSES):
             nc.gpsimd.memset(v_sc[a][:], 0)
         nc.gpsimd.memset(w4_sc[:], 0)
 
-        tab = {}
-        w1_raw = [held([P, PACK, H], F32, "w1_raw0", "slot_b"), held([P, PACK, H], F32, "w1_raw1", "slot_c")]
-        w2_raw = held([P, PASSES, H // 2], I32, "w2_raw")
-        gain_sb = held([P, PACK], F32, "gain_sb")
-
-        def load_tab(a, slot):
-            tab[a] = held([P, T], I32, f"tab{a}", slot)
-            nc.sync.dma_start(out=tab[a][:], in_=tab_words[a].rearrange("p t i -> p (t i)").bitcast(I32))
-
-        nc.sync.dma_start(idx[:], offs)
-        for q in range(QUADS):
-            nc.sync.dma_start(
-                out=tab_sc[32 * q + SC_ROW : 32 * q + 32, :], in_=tab_scales[:, 4 * q : 4 * q + 4, :].bitcast(I32)
-            )
-        load_tab(0, "slot_d")
-        for q in range(QUADS):
-            nc.gpsimd.dma_start(
-                out=w2_sc_raw[32 * q : 32 * q + 4, :, :],
-                in_=w2_scales[:, 4 * q : 4 * q + 4, :].rearrange("a r c -> r a c").bitcast(I32),
-            )
-        for a in range(PASSES):
-            nc.sync.dma_start(
-                out=w1_raw[a][:], in_=w1[a * 512 : (a + 1) * 512, :].rearrange("(p j) c -> p j c", j=PACK)
-            )
-        nc.sync.dma_start(out=w2_raw[:], in_=w2_words.rearrange("a p b -> p a b").bitcast(I32))
-        nc.gpsimd.dma_start(out=gain_sb[:], in_=gain.rearrange("(p t) -> p t", t=PACK))
-        for q in range(QUADS):
-            nc.gpsimd.dma_start(out=w4_sc[32 * q : 32 * q + 4, :], in_=w4_scales[0, 4 * q : 4 * q + 4, :].bitcast(I32))
-
-        identity = held([P, P], F32, "identity")
-        make_identity(nc, identity[:])
-
-        pages, weights = {}, {}
+        tab, pages, weights, crosses, v_codes = {}, {}, {}, {}, {}
         page_rows = page0.rearrange("(p t) c -> t p c", t=PACK)
+        cross_rows = cross.rearrange("(p t) j -> t p j", t=PACK)
         wgs_rows = wgs.rearrange("(m t) j -> m t j", t=PACK)
 
-        def load_page(t, slot):
-            pages[t] = held([P, T2], F32, f"page{t}", slot)
+        def load_tab(a, buffer):
+            tab[a] = held([P, T], I32, f"tab{a}", buffer)
+            nc.sync.dma_start(out=tab[a][:], in_=tab_words[a].rearrange("p t i -> p (t i)").bitcast(I32))
+
+        def load_page(t, buffer):
+            pages[t] = held([P, T2], F32, f"page{t}", buffer)
             nc.sync.dma_start(out=pages[t][:], in_=page_rows[t])
 
-        def load_weight(t, slot):
-            weights[t] = held([P, S], F32, f"weight{t}", slot)
-            for q in (0, 2, 1, 3):
-                nc.sync.dma_start(out=weights[t][32 * q : 32 * q + 32, :], in_=wgs_rows[:, t, :])
-
-        crosses = {}
-        cross_rows = cross.rearrange("(p t) j -> t p j", t=PACK)
+        def load_weight(t, buffer):
+            weights[t] = held([P, S], F32, f"weight{t}", buffer)
+            for q in QUAD_ORDER:
+                nc.sync.dma_start(out=weights[t][QUAD * q : QUAD * (q + 1), :], in_=wgs_rows[:, t, :])
 
         def load_cross(t):
             crosses[t] = held([P, PAIRS], F32, f"cross{t}")
             nc.sync.dma_start(out=crosses[t][:], in_=cross_rows[t])
 
-        halves = S // BANK
-        v_codes = {}
+        w1_raw = [held([P, PACK, H], F32, "w1_raw0", "buffer_b"), held([P, PACK, H], F32, "w1_raw1")]
+        w2_raw = held([P, PASSES, H // 2], I32, "w2_raw")
+        gain_sb = held([P, PACK], F32, "gain_sb")
+        nc.sync.dma_start(idx[:], offs)
+        nc.sync.dma_start(out=tab_sc[SCALE_ROW0:P, :], in_=tab_scales.rearrange("a q t -> (a q) t").bitcast(I32))
+        nc.sync.dma_start(out=w2_raw[:], in_=w2_words.rearrange("a p b -> p a b").bitcast(I32))
+        load_tab(0, "buffer_d")
+        for q in range(QUADS):
+            nc.gpsimd.dma_start(
+                out=w2_sc_raw[QUAD * q : QUAD * q + LIVE, :, :],
+                in_=w2_scales[:, LIVE * q : LIVE * (q + 1), :].rearrange("a r c -> r a c").bitcast(I32),
+            )
+        for a in range(PASSES):
+            nc.sync.dma_start(
+                out=w1_raw[a][:], in_=w1[a * K_PASS : (a + 1) * K_PASS, :].rearrange("(p j) c -> p j c", j=PACK)
+            )
+        nc.gpsimd.dma_start(out=gain_sb[:], in_=gain.rearrange("(p t) -> p t", t=PACK))
+        for q in range(QUADS):
+            nc.gpsimd.dma_start(
+                out=w4_sc[QUAD * q : QUAD * q + LIVE, :], in_=w4_scales[0, LIVE * q : LIVE * (q + 1), :].bitcast(I32)
+            )
+
+        identity = held([P, P], F32, "identity")
+        make_identity(nc, identity[:])
+
+        picked_sc = held([P, S // 4], I32, "picked_sc")
+        nc.vector.tensor_copy(picked_sc[:].bitcast(U8), tab_sc[:].bitcast(U8).indirect(idx[:]))
+
+        def move_scale_rows(group):
+            a, q = divmod(group, QUADS)
+            row = SCALE_ROW0 + LIVE * group
+            nc.sync.dma_start(out=v_sc[a][QUAD * q : QUAD * q + LIVE, :], in_=picked_sc[row : row + LIVE, :])
+
+        for group in range(EARLY_MOVES):
+            move_scale_rows(group)
+        load_tab(1, "buffer_a")
+        for group in range(EARLY_MOVES, PASSES * QUADS):
+            move_scale_rows(group)
+        nc.sync.dma_start(idx2[:], offs2)
 
         def gather_words(a, half):
             v_codes[a, half] = held([P, BANK], U32, f"v_codes{a}{half}")
-            cols = slice(half * BANK // 16, (half + 1) * BANK // 16)
-            nc.vector.tensor_copy(v_codes[a, half][:], tab[a][:].bitcast(U32).indirect(idx[:, cols]))
+            nc.vector.tensor_copy(v_codes[a, half][:], tab[a][:].bitcast(U32).indirect(idx[:, entries(half)]))
 
-        picked_sc = held([P, S // 4], I32, "picked_sc", "slot_e")
-        nc.vector.tensor_copy(picked_sc[:].bitcast(U8), tab_sc[:].bitcast(U8).indirect(idx[:]))
-        for a in range(PASSES):
-            row = SC_ROW + 4 * a
-            nc.sync.dma_start(out=v_sc[a][0:PLANE_ROWS, :], in_=picked_sc[row : row + PLANE_ROWS, :])
-        load_tab(1, "slot_a")
-        nc.sync.dma_start(idx2[:], offs2)
-
-        for half in range(halves):
+        for half in range(HALVES):
             gather_words(0, half)
-        load_page(SLOT_ORDER[0], "slot_d")
+        load_page(SLOT_ORDER[0], "buffer_e")
 
         w1_codes = held([P, PASSES, H], U32, "w1_codes")
         w1_sc = held([P, PASSES, H], U8, "w1_sc")
-        for a in range(PASSES):
-            w1_bf = held([P, PACK * H], BF16, f"w1_bf{a}", ("slot_f", "slot_g")[a])
+        for a, buffer in enumerate(("buffer_f", "buffer_g")):
+            w1_bf = held([P, PACK * H], BF16, f"w1_bf{a}", buffer)
             nc.scalar.copy(
                 out=w1_bf[:].rearrange("p (t m j) -> p m t j", t=PACK, j=PACK),
                 in_=w1_raw[a][:].rearrange("p j (m t) -> p m t j", t=PACK),
@@ -141,7 +148,7 @@ def tile_list_tram_junction_requests_kernel(
             nc.vector.quantize_mx(out=w1_codes[:, a, :].bitcast(FP8X4), scales=w1_sc[:, a, :], in_=w1_bf[:])
 
         w2_codes = held([P, PASSES, 2 * H], U8, "w2_codes")
-        w2_sc = held([P, PASSES, H], U8, "w2_sc", "slot_e")
+        w2_sc = held([P, PASSES, H], U8, "w2_sc", "buffer_d")
         nc.vector.tensor_copy(
             out=w2_codes[:].bitcast(U16).rearrange("p a (t m) -> p a t m", t=PACK),
             in_=w2_raw[:].bitcast(U16).rearrange("p a (m t) -> p a t m", t=PACK),
@@ -151,20 +158,19 @@ def tile_list_tram_junction_requests_kernel(
             in_=w2_sc_raw[:].bitcast(U8).rearrange("p a (m t) -> p a t m", t=PACK),
         )
 
-        for half in range(halves):
+        for half in range(HALVES):
             gather_words(1, half)
 
-        load_weight(SLOT_ORDER[0], "slot_b")
+        load_weight(SLOT_ORDER[0], "buffer_b")
         nc.sync.dma_start(idx4[:], offs4)
         nc.sync.dma_start(idx3[:], offs3)
-        w3_raw = held([P, PACK, N], F32, "w3_raw", "slot_f")
+        w3_raw = held([P, PACK, N], F32, "w3_raw", "buffer_f")
         nc.sync.dma_start(out=w3_raw[:], in_=w3.rearrange("(p j) n -> p j n", j=PACK))
-        load_weight(SLOT_ORDER[1], "slot_g")
-        load_page(SLOT_ORDER[1], "slot_a")
+        load_weight(SLOT_ORDER[1], "buffer_g")
+        load_page(SLOT_ORDER[1], "buffer_a")
         load_cross(SLOT_ORDER[0])
 
-        chunks = T2 // BANK
-        grouped = [held([P, BANK, PACK], BF16, f"grouped{c}") for c in range(chunks)]
+        woven = [held([P, BANK, PACK], BF16, f"woven{c}") for c in range(CHUNKS)]
 
         def products(t, half):
             cols = slice(half * BANK, (half + 1) * BANK)
@@ -215,50 +221,28 @@ def tile_list_tram_junction_requests_kernel(
             nc.scalar.copy(out=target, in_=back[:])
 
         requests = {t: held([P, S], F32, f"request{t}") for t in SLOT_ORDER}
-        t = SLOT_ORDER[0]
-        for half in range(halves):
+        lead = SLOT_ORDER[0]
+        for half in range(HALVES):
             cols = slice(half * BANK, (half + 1) * BANK)
-            part = slice(half * BANK // 16, (half + 1) * BANK // 16)
-            bent, acc2 = products(t, half)
+            bent, acc2 = products(lead, half)
             nc.vector.scalar_tensor_tensor(
-                out=requests[t][:, cols], in0=bent[:], scalar=gain_sb[:, t : t + 1], in1=acc2[:],
+                out=requests[lead][:, cols], in0=bent[:], scalar=gain_sb[:, lead : lead + 1], in1=acc2[:],
                 op0=ALU.mult, op1=ALU.add,
             )
             nc.vector.tensor_tensor(
-                pages[t][:].indirect(idx2[:, part]), requests[t][:, cols], weights[t][:, cols], ALU.mult
+                pages[lead][:].indirect(idx2[:, entries(half)]), requests[lead][:, cols], weights[lead][:, cols],
+                ALU.mult,
             )
         for t in SLOT_ORDER[1:]:
-            for half in range(halves):
+            for half in range(HALVES):
                 bent, acc2 = products(t, half)
                 sum_on_tensor(t, bent, acc2, requests[t][:, half * BANK : (half + 1) * BANK])
 
-        for step, t in enumerate(SLOT_ORDER):
-            page = pages[t]
-            if step > 0:
-                nc.vector.tensor_tensor(page[:].indirect(idx2[:]), requests[t][:], weights[t][:], ALU.mult)
-            if step == 0:
-                w3_bf = held([P, N, PACK], BF16, "w3_bf")
-                w3_codes = held([P, N], U32, "w3_codes")
-                w3_sc = held([P, N], U8, "w3_sc")
-                nc.scalar.copy(
-                    out=w3_bf[:].rearrange("p (n i) j -> p n j i", i=4),
-                    in_=w3_raw[:].rearrange("p j (n i) -> p n j i", i=4),
-                )
-                nc.vector.quantize_mx(
-                    out=w3_codes[:].bitcast(FP8X4), scales=w3_sc[:], in_=w3_bf[:].rearrange("p n j -> p (n j)")
-                )
-                load_page(SLOT_ORDER[2], "slot_f")
-                load_weight(SLOT_ORDER[2], "slot_b")
-                load_cross(SLOT_ORDER[1])
-            if step == 1:
-                load_weight(SLOT_ORDER[3], "slot_g")
-                load_page(SLOT_ORDER[3], "slot_d")
-                load_cross(SLOT_ORDER[2])
-                load_cross(SLOT_ORDER[3])
-            if step == 2:
-                w4_codes = held([P, M], I32, "w4_codes", "slot_b")
-                nc.sync.dma_start(out=w4_codes[:], in_=w4_words[0].rearrange("p c i -> p (c i)").bitcast(I32))
+        def put_requests(t):
+            nc.vector.tensor_tensor(pages[t][:].indirect(idx2[:]), requests[t][:], weights[t][:], ALU.mult)
 
+        def exchange(t):
+            page = pages[t]
             first = work.tile([P, PAIRS], F32, name="first")
             second = work.tile([P, PAIRS], F32, name="second")
             larger = work.tile([P, PAIRS], F32, name="larger")
@@ -269,52 +253,76 @@ def tile_list_tram_junction_requests_kernel(
             nc.vector.tensor_tensor(larger[:], first[:], second[:], ALU.max)
             nc.vector.tensor_tensor(page[:].indirect(idx4[:]), first[:], crossed[:], ALU.add)
             nc.vector.tensor_copy(page[:].indirect(idx3[:]), larger[:])
-            if step < PACK - 1:
-                for c in range(chunks):
-                    nc.scalar.copy(out=grouped[c][:, :, t], in_=page[:, c * BANK : (c + 1) * BANK])
 
-        last = SLOT_ORDER[-1]
-        for c in range(chunks):
-            src = pages[last][:, c * BANK : (c + 1) * BANK]
-            if c % 2 == 0:
-                nc.vector.tensor_copy(out=grouped[c][:, :, last], in_=src)
-            else:
-                nc.scalar.copy(out=grouped[c][:, :, last], in_=src)
-        for c in range(chunks):
-            cols = slice(c * BANK, (c + 1) * BANK)
-            b_codes = work.tile([P, BANK], U32, name="b_codes", bufs=4, align_bytes=64)
-            b_sc = work.tile([P, BANK], U8, name="b_sc", bufs=4, align_bytes=64)
-            nc.vector.quantize_mx(
-                out=b_codes[:].bitcast(FP8X4), scales=b_sc[:], in_=grouped[c][:].rearrange("p c j -> p (c j)")
+        def weave(t, c, copy):
+            copy(out=woven[c][:, :, t], in_=pages[t][:, c * BANK : (c + 1) * BANK])
+
+        def weave_on_scalar(t):
+            for c in range(CHUNKS):
+                weave(t, c, nc.scalar.copy)
+
+        w3_bf = held([P, N, PACK], BF16, "w3_bf")
+        w3_codes = held([P, N], U32, "w3_codes")
+        w3_sc = held([P, N], U8, "w3_sc")
+        nc.scalar.copy(
+            out=w3_bf[:].rearrange("p (n i) j -> p n j i", i=4),
+            in_=w3_raw[:].rearrange("p j (n i) -> p n j i", i=4),
+        )
+        nc.vector.quantize_mx(
+            out=w3_codes[:].bitcast(FP8X4), scales=w3_sc[:], in_=w3_bf[:].rearrange("p n j -> p (n j)")
+        )
+
+        slot_b, slot_c, last = SLOT_ORDER[1:]
+        load_page(slot_c, "buffer_f")
+        load_weight(slot_c, "buffer_b")
+        load_cross(slot_b)
+        exchange(lead)
+        weave_on_scalar(lead)
+
+        put_requests(slot_b)
+        load_weight(last, "buffer_g")
+        load_page(last, "buffer_e")
+        load_cross(slot_c)
+        load_cross(last)
+        exchange(slot_b)
+        weave_on_scalar(slot_b)
+
+        put_requests(slot_c)
+        w4_codes = held([P, M], I32, "w4_codes", "buffer_b")
+        nc.sync.dma_start(out=w4_codes[:], in_=w4_words[0].rearrange("p c i -> p (c i)").bitcast(I32))
+        exchange(slot_c)
+        weave_on_scalar(slot_c)
+
+        put_requests(last)
+        exchange(last)
+        for c in range(CHUNKS):
+            weave(last, c, nc.vector.tensor_copy if c % 2 == 0 else nc.scalar.copy)
+
+        def read_out(codes, scales, block, b_codes, b_sc, tag):
+            acc = psum.tile([P, BANK], F32, name="score", tag=tag)
+            nc.tensor.matmul_mx(
+                out=acc[:],
+                lhsT=codes[:, block * P : (block + 1) * P].bitcast(FP8X4),
+                lhsT_scale=scales[:, block * P : (block + 1) * P],
+                rhs=b_codes[:].bitcast(FP8X4),
+                rhs_scale=b_sc[:],
+                start=True,
+                stop=True,
             )
-            angles, plains = [], []
-            for nb in range(N // P):
-                angle = psum.tile([P, BANK], F32, name="angle", tag="left")
-                nc.tensor.matmul_mx(
-                    out=angle[:],
-                    lhsT=w3_codes[:, nb * P : (nb + 1) * P].bitcast(FP8X4),
-                    lhsT_scale=w3_sc[:, nb * P : (nb + 1) * P],
-                    rhs=b_codes[:].bitcast(FP8X4),
-                    rhs_scale=b_sc[:],
-                    start=True,
-                    stop=True,
-                )
-                angles.append(angle)
-            for mb in range(M // P):
-                plain = psum.tile([P, BANK], F32, name="plain", tag="right")
-                nc.tensor.matmul_mx(
-                    out=plain[:],
-                    lhsT=w4_codes[:, mb * P : (mb + 1) * P].bitcast(FP8X4),
-                    lhsT_scale=w4_sc[:].bitcast(U8)[:, mb * P : (mb + 1) * P],
-                    rhs=b_codes[:].bitcast(FP8X4),
-                    rhs_scale=b_sc[:],
-                    start=True,
-                    stop=True,
-                )
-                plains.append(plain)
+            return acc
+
+        for c in range(CHUNKS):
+            cols = slice(c * BANK, (c + 1) * BANK)
+            b_codes = work.tile([P, BANK], U32, name="b_codes", bufs=CHUNKS, align_bytes=64)
+            b_sc = work.tile([P, BANK], U8, name="b_sc", bufs=CHUNKS, align_bytes=64)
+            nc.vector.quantize_mx(
+                out=b_codes[:].bitcast(FP8X4), scales=b_sc[:], in_=woven[c][:].rearrange("p c j -> p (c j)")
+            )
+            angles = [read_out(w3_codes, w3_sc[:], nb, b_codes, b_sc, "left") for nb in range(N // P)]
+            plains = [read_out(w4_codes, w4_sc[:].bitcast(U8), mb, b_codes, b_sc, "right") for mb in range(M // P)]
             turns = []
             for angle in angles:
-                turn = work.tile([P, BANK], I32, name="turn", bufs=2)
+                turn = work.tile([P, BANK], I32, name="turn")
                 nc.vector.tensor_scalar(turn[:], angle[:], 1.0 / (2.0 * math.pi), None, ALU.mult)
                 turns.append(turn)
             for mb, plain in enumerate(plains):

import math
from contextlib import ExitStack

import concourse.mybir as mybir
from concourse.masks import make_identity

K, H, N, M, T, S, T2, PAIRS = 1024, 512, 256, 256, 4096, 1024, 2048, 512
FLOPS = 2 * (2 * K * H * S + H * (N + M) * T2)

F32 = mybir.dt.float32
BF16 = mybir.dt.bfloat16
I32 = mybir.dt.int32
U32 = mybir.dt.uint32
U16 = mybir.dt.uint16
U8 = mybir.dt.uint8
FP8X4 = mybir.dt.float8_e4m3fn_x4
FP4X4 = mybir.dt.float4_e2m1fn_x4
ALU = mybir.AluOpType
ACT = mybir.ActivationFunctionType

P = 128
PACK = 4
K_PASS = P * PACK
PASSES = K // K_PASS
BANK = 512
QUADS = 4
QUAD = P // QUADS
LIVE = 4
PER_COLUMN = 16
HALVES = S // BANK
CHUNKS = T2 // BANK
SCALE_ROW0 = P - PASSES * QUADS * LIVE
EARLY_MOVES = 6
SLOT_ORDER = (2, 0, 1, 3)
QUAD_ORDER = (0, 2, 1, 3)


def tile_list_tram_junction_requests_kernel(
    tc, tab_words, tab_scales, offs, offs2, offs3, offs4, w1, gain, w2_words, w2_scales,
    page0, wgs, cross, w3, w4_words, w4_scales, out,
):
    nc = tc.nc
    with ExitStack() as ctx:
        lists = ctx.enter_context(tc.tile_pool(name="lists", bufs=1))
        keep = ctx.enter_context(tc.tile_pool(name="keep", bufs=1))
        work = ctx.enter_context(tc.tile_pool(name="work", bufs=2))
        psum = ctx.enter_context(tc.psum_pool(name="psum", bufs=4))

        def held(shape, dtype, name, buffer=""):
            return keep.tile(shape, dtype, name=name, tag=buffer or name, align_bytes=64)

        def entries(half):
            return slice(half * BANK // PER_COLUMN, (half + 1) * BANK // PER_COLUMN)

        idx = lists.tile([P, S // PER_COLUMN], U16, name="idx")
        idx2 = lists.tile([P, S // PER_COLUMN], U16, name="idx2")
        idx3 = lists.tile([P, PAIRS // PER_COLUMN], U16, name="idx3")
        idx4 = lists.tile([P, PAIRS // PER_COLUMN], U16, name="idx4")

        tab_sc = held([P, T // 4], I32, "tab_sc", "buffer_e")
        w2_sc_raw = held([P, PASSES, H // 4], I32, "w2_sc_raw")
        v_sc = [held([P, S // 4], I32, f"v_sc{a}") for a in range(PASSES)]
        w4_sc = held([P, M // 4], I32, "w4_sc")
        nc.vector.memset(tab_sc[0:SCALE_ROW0, :], 0)
        nc.gpsimd.memset(w2_sc_raw[:], 0)
        for a in range(PASSES):
            nc.gpsimd.memset(v_sc[a][:], 0)
        nc.gpsimd.memset(w4_sc[:], 0)

        tab, pages, weights, crosses, v_codes = {}, {}, {}, {}, {}
        page_rows = page0.rearrange("(p t) c -> t p c", t=PACK)
        cross_rows = cross.rearrange("(p t) j -> t p j", t=PACK)
        wgs_rows = wgs.rearrange("(m t) j -> m t j", t=PACK)

        def load_tab(a, buffer):
            tab[a] = held([P, T], I32, f"tab{a}", buffer)
            nc.sync.dma_start(out=tab[a][:], in_=tab_words[a].rearrange("p t i -> p (t i)").bitcast(I32))

        def load_page(t, buffer):
            pages[t] = held([P, T2], F32, f"page{t}", buffer)
            nc.sync.dma_start(out=pages[t][:], in_=page_rows[t])

        def load_weight(t, buffer):
            weights[t] = held([P, S], F32, f"weight{t}", buffer)
            for q in QUAD_ORDER:
                nc.sync.dma_start(out=weights[t][QUAD * q : QUAD * (q + 1), :], in_=wgs_rows[:, t, :])

        def load_cross(t):
            crosses[t] = held([P, PAIRS], F32, f"cross{t}")
            nc.sync.dma_start(out=crosses[t][:], in_=cross_rows[t])

        w1_raw = [held([P, PACK, H], F32, "w1_raw0", "buffer_b"), held([P, PACK, H], F32, "w1_raw1")]
        w2_raw = held([P, PASSES, H // 2], I32, "w2_raw")
        gain_sb = held([P, PACK], F32, "gain_sb")
        nc.sync.dma_start(idx[:], offs)
        nc.sync.dma_start(out=tab_sc[SCALE_ROW0:P, :], in_=tab_scales.rearrange("a q t -> (a q) t").bitcast(I32))
        nc.sync.dma_start(out=w2_raw[:], in_=w2_words.rearrange("a p b -> p a b").bitcast(I32))
        load_tab(0, "buffer_d")
        for q in range(QUADS):
            nc.gpsimd.dma_start(
                out=w2_sc_raw[QUAD * q : QUAD * q + LIVE, :, :],
                in_=w2_scales[:, LIVE * q : LIVE * (q + 1), :].rearrange("a r c -> r a c").bitcast(I32),
            )
        for a in range(PASSES):
            nc.sync.dma_start(
                out=w1_raw[a][:], in_=w1[a * K_PASS : (a + 1) * K_PASS, :].rearrange("(p j) c -> p j c", j=PACK)
            )
        nc.gpsimd.dma_start(out=gain_sb[:], in_=gain.rearrange("(p t) -> p t", t=PACK))
        for q in range(QUADS):
            nc.gpsimd.dma_start(
                out=w4_sc[QUAD * q : QUAD * q + LIVE, :], in_=w4_scales[0, LIVE * q : LIVE * (q + 1), :].bitcast(I32)
            )

        identity = held([P, P], F32, "identity")
        make_identity(nc, identity[:])

        picked_sc = held([P, S // 4], I32, "picked_sc")
        nc.vector.tensor_copy(picked_sc[:].bitcast(U8), tab_sc[:].bitcast(U8).indirect(idx[:]))

        def move_scale_rows(group):
            a, q = divmod(group, QUADS)
            row = SCALE_ROW0 + LIVE * group
            nc.sync.dma_start(out=v_sc[a][QUAD * q : QUAD * q + LIVE, :], in_=picked_sc[row : row + LIVE, :])

        for group in range(EARLY_MOVES):
            move_scale_rows(group)
        load_tab(1, "buffer_a")
        for group in range(EARLY_MOVES, PASSES * QUADS):
            move_scale_rows(group)
        nc.sync.dma_start(idx2[:], offs2)

        def gather_words(a, half):
            v_codes[a, half] = held([P, BANK], U32, f"v_codes{a}{half}")
            nc.vector.tensor_copy(v_codes[a, half][:], tab[a][:].bitcast(U32).indirect(idx[:, entries(half)]))

        for half in range(HALVES):
            gather_words(0, half)
        load_page(SLOT_ORDER[0], "buffer_e")

        w1_codes = held([P, PASSES, H], U32, "w1_codes")
        w1_sc = held([P, PASSES, H], U8, "w1_sc")
        for a, buffer in enumerate(("buffer_f", "buffer_g")):
            w1_bf = held([P, PACK * H], BF16, f"w1_bf{a}", buffer)
            nc.scalar.copy(
                out=w1_bf[:].rearrange("p (t m j) -> p m t j", t=PACK, j=PACK),
                in_=w1_raw[a][:].rearrange("p j (m t) -> p m t j", t=PACK),
            )
            nc.vector.quantize_mx(out=w1_codes[:, a, :].bitcast(FP8X4), scales=w1_sc[:, a, :], in_=w1_bf[:])

        w2_codes = held([P, PASSES, 2 * H], U8, "w2_codes")
        w2_sc = held([P, PASSES, H], U8, "w2_sc", "buffer_d")
        nc.vector.tensor_copy(
            out=w2_codes[:].bitcast(U16).rearrange("p a (t m) -> p a t m", t=PACK),
            in_=w2_raw[:].bitcast(U16).rearrange("p a (m t) -> p a t m", t=PACK),
        )
        nc.vector.tensor_copy(
            out=w2_sc[:].rearrange("p a (t m) -> p a t m", t=PACK),
            in_=w2_sc_raw[:].bitcast(U8).rearrange("p a (m t) -> p a t m", t=PACK),
        )

        for half in range(HALVES):
            gather_words(1, half)

        load_weight(SLOT_ORDER[0], "buffer_b")
        nc.sync.dma_start(idx4[:], offs4)
        nc.sync.dma_start(idx3[:], offs3)
        w3_raw = held([P, PACK, N], F32, "w3_raw", "buffer_f")
        nc.sync.dma_start(out=w3_raw[:], in_=w3.rearrange("(p j) n -> p j n", j=PACK))
        load_weight(SLOT_ORDER[1], "buffer_g")
        load_page(SLOT_ORDER[1], "buffer_a")
        load_cross(SLOT_ORDER[0])

        woven = [held([P, BANK, PACK], BF16, f"woven{c}") for c in range(CHUNKS)]

        def products(t, half):
            cols = slice(half * BANK, (half + 1) * BANK)
            acc1 = psum.tile([P, BANK], F32, name="acc1", tag="left")
            acc2 = psum.tile([P, BANK], F32, name="acc2", tag="right")
            for a in range(PASSES):
                nc.tensor.matmul_mx(
                    out=acc1[:],
                    lhsT=w1_codes[:, a, t * P : (t + 1) * P].bitcast(FP8X4),
                    lhsT_scale=w1_sc[:, a, t * P : (t + 1) * P],
                    rhs=v_codes[a, half][:].bitcast(FP8X4),
                    rhs_scale=v_sc[a][:].bitcast(U8)[:, cols],
                    start=(a == 0),
                    stop=(a == PASSES - 1),
                )
            for a in range(PASSES):
                nc.tensor.matmul_mx(
                    out=acc2[:],
                    lhsT=w2_codes[:, a, 2 * t * P : 2 * (t + 1) * P].bitcast(FP4X4),
                    lhsT_scale=w2_sc[:, a, t * P : (t + 1) * P],
                    rhs=v_codes[a, half][:].bitcast(FP8X4),
                    rhs_scale=v_sc[a][:].bitcast(U8)[:, cols],
                    start=(a == 0),
                    stop=(a == PASSES - 1),
                )
            bent = work.tile([P, BANK], F32, name="bent", bufs=3)
            nc.scalar.activation(out=bent[:], in_=acc1[:], func=ACT.Tanh)
            return bent, acc2

        def sum_on_tensor(t, bent, acc2, target):
            gained = work.tile([P, BANK], F32, name="gained")
            linear = work.tile([P, BANK], F32, name="linear")
            turned = work.tile([P, BANK], F32, name="turned")
            nc.scalar.activation(out=gained[:], in_=bent[:], func=ACT.Copy, scale=gain_sb[:, t : t + 1])
            nc.scalar.copy(out=linear[:], in_=acc2[:])
            summed = psum.tile([P, BANK], F32, name="summed", tag="left")
            for blk in range(BANK // P):
                cols = slice(blk * P, (blk + 1) * P)
                for term, opens in ((gained, True), (linear, False)):
                    nc.tensor.matmul(
                        summed[:, cols], term[:, cols], identity[:], start=opens, stop=not opens, is_transpose=True
                    )
            nc.scalar.copy(out=turned[:], in_=summed[:])
            back = psum.tile([P, BANK], F32, name="back", tag="right")
            for blk in range(BANK // P):
                cols = slice(blk * P, (blk + 1) * P)
                nc.tensor.transpose(back[:, cols], turned[:, cols], identity[:])
            nc.scalar.copy(out=target, in_=back[:])

        requests = {t: held([P, S], F32, f"request{t}") for t in SLOT_ORDER}
        lead = SLOT_ORDER[0]
        for half in range(HALVES):
            cols = slice(half * BANK, (half + 1) * BANK)
            bent, acc2 = products(lead, half)
            nc.vector.scalar_tensor_tensor(
                out=requests[lead][:, cols], in0=bent[:], scalar=gain_sb[:, lead : lead + 1], in1=acc2[:],
                op0=ALU.mult, op1=ALU.add,
            )
            nc.vector.tensor_tensor(
                pages[lead][:].indirect(idx2[:, entries(half)]), requests[lead][:, cols], weights[lead][:, cols],
                ALU.mult,
            )
        for t in SLOT_ORDER[1:]:
            for half in range(HALVES):
                bent, acc2 = products(t, half)
                sum_on_tensor(t, bent, acc2, requests[t][:, half * BANK : (half + 1) * BANK])

        def put_requests(t):
            nc.vector.tensor_tensor(pages[t][:].indirect(idx2[:]), requests[t][:], weights[t][:], ALU.mult)

        def exchange(t):
            page = pages[t]
            first = work.tile([P, PAIRS], F32, name="first")
            second = work.tile([P, PAIRS], F32, name="second")
            larger = work.tile([P, PAIRS], F32, name="larger")
            crossed = work.tile([P, PAIRS], F32, name="crossed")
            nc.vector.tensor_copy(second[:], page[:].indirect(idx4[:]))
            nc.vector.tensor_copy(first[:], page[:].indirect(idx3[:]))
            nc.vector.tensor_tensor(crossed[:], second[:], crosses[t][:], ALU.mult)
            nc.vector.tensor_tensor(larger[:], first[:], second[:], ALU.max)
            nc.vector.tensor_tensor(page[:].indirect(idx4[:]), first[:], crossed[:], ALU.add)
            nc.vector.tensor_copy(page[:].indirect(idx3[:]), larger[:])

        def weave(t, c, copy):
            copy(out=woven[c][:, :, t], in_=pages[t][:, c * BANK : (c + 1) * BANK])

        def weave_on_scalar(t):
            for c in range(CHUNKS):
                weave(t, c, nc.scalar.copy)

        w3_bf = held([P, N, PACK], BF16, "w3_bf")
        w3_codes = held([P, N], U32, "w3_codes")
        w3_sc = held([P, N], U8, "w3_sc")
        nc.scalar.copy(
            out=w3_bf[:].rearrange("p (n i) j -> p n j i", i=4),
            in_=w3_raw[:].rearrange("p j (n i) -> p n j i", i=4),
        )
        nc.vector.quantize_mx(
            out=w3_codes[:].bitcast(FP8X4), scales=w3_sc[:], in_=w3_bf[:].rearrange("p n j -> p (n j)")
        )

        slot_b, slot_c, last = SLOT_ORDER[1:]
        load_page(slot_c, "buffer_f")
        load_weight(slot_c, "buffer_b")
        load_cross(slot_b)
        exchange(lead)
        weave_on_scalar(lead)

        put_requests(slot_b)
        load_weight(last, "buffer_g")
        load_page(last, "buffer_e")
        load_cross(slot_c)
        load_cross(last)
        exchange(slot_b)
        weave_on_scalar(slot_b)

        put_requests(slot_c)
        w4_codes = held([P, M], I32, "w4_codes", "buffer_b")
        nc.sync.dma_start(out=w4_codes[:], in_=w4_words[0].rearrange("p c i -> p (c i)").bitcast(I32))
        exchange(slot_c)
        weave_on_scalar(slot_c)

        put_requests(last)
        exchange(last)
        for c in range(CHUNKS):
            weave(last, c, nc.vector.tensor_copy if c % 2 == 0 else nc.scalar.copy)

        def read_out(codes, scales, block, b_codes, b_sc, tag):
            acc = psum.tile([P, BANK], F32, name="score", tag=tag)
            nc.tensor.matmul_mx(
                out=acc[:],
                lhsT=codes[:, block * P : (block + 1) * P].bitcast(FP8X4),
                lhsT_scale=scales[:, block * P : (block + 1) * P],
                rhs=b_codes[:].bitcast(FP8X4),
                rhs_scale=b_sc[:],
                start=True,
                stop=True,
            )
            return acc

        for c in range(CHUNKS):
            cols = slice(c * BANK, (c + 1) * BANK)
            b_codes = work.tile([P, BANK], U32, name="b_codes", bufs=CHUNKS, align_bytes=64)
            b_sc = work.tile([P, BANK], U8, name="b_sc", bufs=CHUNKS, align_bytes=64)
            nc.vector.quantize_mx(
                out=b_codes[:].bitcast(FP8X4), scales=b_sc[:], in_=woven[c][:].rearrange("p c j -> p (c j)")
            )
            angles = [read_out(w3_codes, w3_sc[:], nb, b_codes, b_sc, "left") for nb in range(N // P)]
            plains = [read_out(w4_codes, w4_sc[:].bitcast(U8), mb, b_codes, b_sc, "right") for mb in range(M // P)]
            turns = []
            for angle in angles:
                turn = work.tile([P, BANK], I32, name="turn")
                nc.vector.tensor_scalar(turn[:], angle[:], 1.0 / (2.0 * math.pi), None, ALU.mult)
                turns.append(turn)
            for mb, plain in enumerate(plains):
                staged = work.tile([P, BANK], F32, name="staged", bufs=6)
                nc.scalar.copy(out=staged[:], in_=plain[:])
                nc.sync.dma_start(out=out[N + mb * P : N + (mb + 1) * P, cols], in_=staged[:])
            for nb, angle in enumerate(angles):
                wrapped = work.tile([P, BANK], F32, name="wrapped", bufs=3)
                nc.vector.scalar_tensor_tensor(
                    out=wrapped[:], in0=turns[nb][:], scalar=-2.0 * math.pi, in1=angle[:], op0=ALU.mult, op1=ALU.add
                )
                staged = work.tile([P, BANK], F32, name="staged", bufs=6)
                nc.scalar.activation(out=staged[:], in_=wrapped[:], func=ACT.Sin)
                nc.sync.dma_start(out=out[nb * P : (nb + 1) * P, cols], in_=staged[:])
